import numpy as np
import ml_dtypes


def mxq(x, axis, fmt="e4m3"):
    dtype, down = {"e4m3": (ml_dtypes.float8_e4m3fn, 7), "e5m2": (ml_dtypes.float8_e5m2, 14)}[fmt]
    v = np.moveaxis(np.asarray(x, np.float32).astype(ml_dtypes.bfloat16).astype(np.float64), axis, -1)
    blocks = v.reshape(v.shape[:-1] + (-1, 32))
    amax = np.abs(blocks).max(-1, keepdims=True)
    byte = np.maximum(np.where(amax > 0, np.frexp(amax)[1] - 1 + 127, 0) - down, 1)
    scale = np.exp2(byte - 127.0)
    codes = (blocks / scale).astype(np.float32).astype(dtype).astype(np.float64)
    return np.moveaxis((codes * scale).reshape(v.shape), -1, axis)


WIDE = False


def mx_kscale(k):
    if not WIDE:
        return np.ones(k)
    levels = np.array([30, -30])
    if k % 512:
        return np.exp2(np.random.permutation(np.resize(levels, k // 32))).repeat(32)
    a = np.empty((k // 512, 16))
    for p in range(k // 512):
        a[p, :8] = np.random.permutation(np.resize(levels, 8))
        for g in range(8):
            far = levels[np.abs(levels - a[p, g]) >= 10]
            a[p, g + 8] = far[np.random.randint(len(far))]
    return np.exp2(a.ravel()).repeat(32)


def f64(x):
    return np.asarray(x).astype(np.float64)


def striped(idx):
    return np.tile(np.asarray(idx).reshape(-1, 16).T, (8, 1)).astype(np.uint16)


def unstriped(offs):
    return offs[:16].T.reshape(-1).astype(np.int64)


E2M1 = np.array([0.0, 0.5, 1.0, 1.5, 2.0, 3.0, 4.0, 6.0, -0.0, -0.5, -1.0, -1.5, -2.0, -3.0, -4.0, -6.0])


def pack_weight(w, fmt):
    k, n = w.shape
    w = f64(np.asarray(w, np.float32).astype(ml_dtypes.bfloat16)).reshape(k // 32, 32, n)
    amax = np.abs(w).max(1)
    if fmt in ("e4m3", "e5m2"):
        byte = np.frexp(amax)[1] - 1 + 127 - (7 if fmt == "e4m3" else 14)
    else:
        mant, ex = np.frexp(amax / 6.0)
        byte = np.where(mant > 0.5, ex, ex - 1) + 127
    byte = np.clip(np.where(amax > 0, byte, 1), 1, 254)
    scaled = (w * np.exp2(127.0 - byte)[:, None, :]).reshape(k, n).astype(np.float32)
    by_word = np.ascontiguousarray(scaled.reshape(k // 512, 128, 4, n).transpose(0, 1, 3, 2))
    if fmt in ("e4m3", "e5m2"):
        words = by_word.astype(ml_dtypes.float8_e4m3fn if fmt == "e4m3" else ml_dtypes.float8_e5m2).view(np.uint8)
    else:
        c = by_word.astype(ml_dtypes.float4_e2m1fn).view(np.uint8) & 0xF
        words = (c[..., 0::2] | (c[..., 1::2] << 4)).reshape(k // 512, 128, 2 * n)
    return np.ascontiguousarray(words), np.ascontiguousarray(byte.astype(np.uint8).reshape(k // 512, 16, n))


def unpack_weight(words, scales, fmt):
    g, _, n = scales.shape
    words = np.ascontiguousarray(words).reshape(g, 128, n, -1)
    if fmt in ("e4m3", "e5m2"):
        vals = words.view(ml_dtypes.float8_e4m3fn if fmt == "e4m3" else ml_dtypes.float8_e5m2).astype(np.float64)
    else:
        nib = np.empty((g, 128, n, 4), np.uint8)
        nib[..., 0::2] = words & 0xF
        nib[..., 1::2] = words >> 4
        vals = E2M1[nib]
    vals = vals * np.repeat(np.exp2(scales.astype(np.float64) - 127.0), 8, axis=1)[..., None]
    return vals.transpose(0, 1, 3, 2).reshape(g * 512, n)


def sigmoid(v):
    return 1.0 / (1.0 + np.exp(-v))


K, T, J, R, O, N, L = 512, 1024, 256, 512, 128, 256, 512


def setup_inputs():
    n = np.random.standard_normal
    idx = np.random.permutation(T)[:J]
    idx2 = np.random.permutation(J)[:O]
    idx3 = np.random.permutation(J)[:O]
    fk = mx_kscale(K)
    fr = mx_kscale(R)
    fl = mx_kscale(L)
    xtp = pack_weight(n((K, T)) / fk[:, None], "e2m1")
    wp = pack_weight(n((K, R)) * 1 / np.sqrt(K) * fk[:, None], "e5m2")
    w2p = pack_weight(n((K, R)) * 1 / np.sqrt(K) * fk[:, None] * fr, "e4m3")
    wbp = pack_weight(n((R, N)) * 1 / np.sqrt(R) / fr[:, None], "e4m3")
    sxp = pack_weight(n((L, O)) / fl[:, None], "e5m2")
    wsp = pack_weight(n((L, N)) * 1 / np.sqrt(L) * fl[:, None], "e4m3")
    return {
        "xt_words": xtp[0],
        "xt_scales": xtp[1],
        "w_words": wp[0],
        "w_scales": wp[1],
        "w2_words": w2p[0],
        "w2_scales": w2p[1],
        "sg": (np.random.uniform(0.6, 1.6, (R, 1))).astype(np.float32),
        "wb_words": wbp[0],
        "wb_scales": wbp[1],
        "sx_words": sxp[0],
        "sx_scales": sxp[1],
        "ws_words": wsp[0],
        "ws_scales": wsp[1],
        "offs": striped(idx),
        "offs2": striped(idx2),
        "offs3": striped(idx3),
    }


def reference(xt_words, xt_scales, w_words, w_scales, w2_words, w2_scales, sg, wb_words, wb_scales, sx_words, sx_scales, ws_words, ws_scales, offs, offs2, offs3):
    idx = unstriped(offs)
    idx2 = unstriped(offs2)
    idx3 = unstriped(offs3)
    xtu = unpack_weight(xt_words, xt_scales, "e2m1")
    wu = unpack_weight(w_words, w_scales, "e5m2")
    w2u = unpack_weight(w2_words, w2_scales, "e4m3")
    wbu = unpack_weight(wb_words, wb_scales, "e4m3")
    sxu = unpack_weight(sx_words, sx_scales, "e5m2")
    wsu = unpack_weight(ws_words, ws_scales, "e4m3")
    xtidxg = xtu[:, idx]
    a = wu.T @ xtidxg
    b = w2u.T @ xtidxg
    hid = np.maximum(b[:, idx2], b[:, idx3]) * sigmoid(a[:, idx3] * f64(sg))
    hidq = mxq(hid, 0, "e5m2")
    y = wbu.T @ hidq + wsu.T @ sxu
    return y

@@ -1,0 +1,208 @@
+from contextlib import ExitStack
+
+import concourse.mybir as mybir
+
+F32 = mybir.dt.float32
+BF16 = mybir.dt.bfloat16
+I32 = mybir.dt.int32
+U32 = mybir.dt.uint32
+U16 = mybir.dt.uint16
+U8 = mybir.dt.uint8
+E4M3 = mybir.dt.float8_e4m3fn_x4
+E5M2 = mybir.dt.float8_e5m2_x4
+E2M1 = mybir.dt.float4_e2m1fn_x4
+ACT = mybir.ActivationFunctionType
+ALU = mybir.AluOpType
+
+K, T, J, R, O, N, L = 512, 1024, 256, 512, 128, 256, 512
+P = 128
+PACK = 4
+FLOPS = 2 * (2 * K * R * J + R * N * O + L * N * O)
+
+
+def tile_list_twow_agree_skip_plain_kernel(tc, xt_words, xt_scales, w_words, w_scales, w2_words, w2_scales, sg,
+                                                 wb_words, wb_scales, sx_words, sx_scales, ws_words, ws_scales,
+                                                 offs, offs2, offs3, out):
+    nc = tc.nc
+    with ExitStack() as ctx:
+        keep = ctx.enter_context(tc.tile_pool(name="keep", bufs=1))
+        psum = ctx.enter_context(tc.psum_pool(name="psum", bufs=8))
+
+        def sb(name, cols, dtype, tag=None):
+            return keep.tile([P, cols], dtype, name=name, tag=tag or name, align_bytes=64)
+
+        list1 = keep.tile([P, J // 16], U16, name="list1")
+        list2 = keep.tile([P, O // 16], U16, name="list2")
+        list3 = keep.tile([P, O // 16], U16, name="list3")
+        xt_w = sb("xt_w", T, U16)
+        xt_s = sb("xt_s", T, U8)
+        w_w = sb("w_w", R, U32)
+        w_s = sb("w_s", R, U8)
+        w2_w = sb("w2_w", R, U32)
+        w2_s = sb("w2_s", R, U8)
+        wb_w = sb("wb_w", N, U32)
+        wb_s = sb("wb_s", N, U8)
+        ws_w = sb("ws_w", N, U32)
+        ws_s = sb("ws_s", N, U8)
+        sx_w = sb("sx_w", O, U32)
+        sx_s = sb("sx_s", O, U8)
+        slope = sb("slope", PACK, F32)
+
+        def load_words(queue, tile, words):
+            queue.dma_start(out=tile[:].bitcast(I32), in_=words[0].rearrange("p n t -> p (n t)").bitcast(I32))
+
+        def spread_scales(queues, tile, scales):
+            for q in range(4):
+                rows = scales[0, 4 * q : 4 * q + 4, :].bitcast(I32)
+                queues[q].dma_start(out=tile[32 * q : 32 * q + 32, :].bitcast(I32),
+                                    in_=rows.unsqueeze(0).to_broadcast([8, 4, rows.shape[1]]))
+
+        def load_scales(queues, tile, scales):
+            for q in range(4):
+                queues[q].dma_start(out=tile[32 * q : 32 * q + 4, :].bitcast(I32),
+                                    in_=scales[0, 4 * q : 4 * q + 4, :].bitcast(I32))
+
+        for plane in (ws_s, sx_s, wb_s):
+            nc.vector.memset(plane[:].bitcast(I32), 0)
+        S, A, G = nc.sync, nc.scalar, nc.gpsimd
+        spread_scales((S, A, S, A), xt_s, xt_scales)
+        S.dma_start(list1[:], offs)
+        A.dma_start(out=xt_w[:].bitcast(I32), in_=xt_words[0].bitcast(I32))
+        load_words(A, w2_w, w2_words)
+        load_words(A, w_w, w_words)
+        spread_scales((S, S, S, S), w2_s, w2_scales)
+        S.dma_start(list2[:], offs2)
+        S.dma_start(list3[:], offs3)
+        spread_scales((G, G, S, S), w_s, w_scales)
+        G.dma_start(out=slope[:], in_=sg.rearrange("(p t) one -> p (t one)", t=PACK))
+        load_words(S, ws_w, ws_words)
+        load_words(S, sx_w, sx_words)
+        load_words(S, wb_w, wb_words)
+        load_scales((S, S, S, S), ws_s, ws_scales)
+        load_scales((S, S, S, S), sx_s, sx_scales)
+        load_scales((S, S, S, S), wb_s, wb_scales)
+
+        xg_w = sb("xg_w", J, U16)
+        xg_s = sb("xg_s", J, U8)
+        wd_w = sb("wd_w", R, U32)
+        wd_s = sb("wd_s", R, U8)
+        w2d_w = sb("w2d_w", R, U32)
+        w2d_s = sb("w2d_s", R, U8)
+
+        def deal_views(dst, src, run):
+            return (dst.rearrange("p (t c i) -> p c t i", t=PACK, i=run),
+                    src.rearrange("p (c i t) -> p c t i", t=PACK, i=run))
+
+        def deal_words_scalar(dst, src):
+            d, s = deal_views(dst[:], src[:], 4)
+            nc.scalar.copy(out=d, in_=s)
+
+        def deal_words_vector(dst, src):
+            d, s = deal_views(dst[:].bitcast(I32), src[:].bitcast(I32), 4)
+            nc.vector.tensor_copy(out=d, in_=s)
+
+        def deal_scales(engine, dst, src):
+            d, s = deal_views(dst[:], src[:], 16)
+            engine.tensor_copy(out=d, in_=s)
+
+        nc.vector.tensor_copy(out=xg_s[:], in_=xt_s[:].indirect(list1[:]))
+        nc.vector.tensor_copy(out=xg_w[:], in_=xt_w[:].indirect(list1[:]))
+        deal_words_scalar(w2d_w, w2_w)
+        deal_scales(nc.vector, w2d_s, w2_s)
+        deal_words_vector(wd_w, w_w)
+        deal_scales(nc.vector, wd_s, w_s)
+
+        def first_stage(name, words, scales, fmt, t):
+            acc = psum.tile([P, J], F32, name=name, tag="acc")
+            cols = slice(P * t, P * (t + 1))
+            nc.tensor.matmul_mx(out=acc[:], lhsT=words[:, cols].bitcast(fmt), lhsT_scale=scales[:, cols],
+                                rhs=xg_w[:].bitcast(E2M1), rhs_scale=xg_s[:], start=True, stop=True)
+            return acc
+
+        def leave_psum(on_scalar, dst, src):
+            if on_scalar:
+                nc.scalar.copy(out=dst, in_=src)
+            else:
+                nc.vector.tensor_copy(out=dst, in_=src)
+
+        def pick(on_scalar, dst, window, offsets):
+            if on_scalar:
+                nc.scalar.activation(out=dst, in_=window[:].indirect(offsets[:]), func=ACT.Copy)
+            else:
+                nc.vector.tensor_copy(out=dst, in_=window[:].indirect(offsets[:]))
+
+        a_sb = [sb("a_sb%d" % t, J, F32) for t in range(PACK)]
+        b_sb = [sb("b_sb%d" % t, J, F32) for t in range(PACK)]
+        picked = sb("picked", 2 * PACK * O, F32, "w_s")
+        b2 = [picked[:, O * t : O * (t + 1)] for t in range(PACK)]
+        b3 = [picked[:, O * (PACK + t) : O * (PACK + t + 1)] for t in range(PACK)]
+        gate = sb("gate", PACK * O, F32)
+        top = sb("top", PACK * O, F32)
+        a_ps = {}
+        b_ps = {}
+
+        def mm_a(t):
+            a_ps[t] = first_stage("a_ps%d" % t, wd_w, wd_s, E5M2, t)
+
+        def mm_b(t):
+            b_ps[t] = first_stage("b_ps%d" % t, w2d_w, w2d_s, E4M3, t)
+
+        def out_a(t, on_scalar):
+            leave_psum(on_scalar, a_sb[t][:], a_ps[t][:])
+
+        def out_b(t, on_scalar):
+            leave_psum(on_scalar, b_sb[t][:], b_ps[t][:])
+
+        def look(t):
+            nc.scalar.activation(out=gate[:, O * t : O * (t + 1)], in_=a_sb[t][:].indirect(list3[:]),
+                                 func=ACT.Sigmoid, scale=slope[:, t : t + 1])
+
+        def pick2(t, on_scalar):
+            pick(on_scalar, b2[t], b_sb[t], list2)
+
+        def pick3(t, on_scalar):
+            pick(on_scalar, b3[t], b_sb[t], list3)
+
+        def larger(t):
+            nc.vector.tensor_tensor(out=top[:, O * t : O * (t + 1)], in0=b2[t], in1=b3[t], op=ALU.max)
+
+        for t in range(PACK):
+            mm_b(t)
+        for t in range(PACK):
+            mm_a(t)
+        for t in range(PACK):
+            out_b(t, True)
+            pick2(t, False)
+            pick3(t, False)
+            larger(t)
+        for t in range(PACK):
+            out_a(t, True)
+            look(t)
+
+        hid = sb("hid", PACK * O, BF16)
+        hq_w = sb("hq_w", O, U32)
+        hq_s = sb("hq_s", O, U8)
+        y_ps = []
+        for h in range(N // P):
+            acc = psum.tile([P, O], F32, name="y_ps%d" % h, tag="acc")
+            cols = slice(P * h, P * (h + 1))
+            nc.tensor.matmul_mx(out=acc[:], lhsT=ws_w[:, cols].bitcast(E4M3), lhsT_scale=ws_s[:, cols],
+                                rhs=sx_w[:].bitcast(E5M2), rhs_scale=sx_s[:], start=True, stop=False)
+            y_ps.append(acc)
+        hid_v = hid[:].rearrange("p (c i t) -> p c t i", t=PACK, i=4)
+        top_v = top[:].rearrange("p (t c i) -> p c t i", t=PACK, i=4)
+        gate_v = gate[:].rearrange("p (t c i) -> p c t i", t=PACK, i=4)
+        for u in range(2):
+            part = slice(16 * u, 16 * (u + 1))
+            nc.vector.tensor_tensor(out=hid_v[:, part], in0=top_v[:, part], in1=gate_v[:, part], op=ALU.mult)
+        for u in range(2):
+            nc.vector.quantize_mx(out=hq_w[:, 64 * u : 64 * (u + 1)].bitcast(E5M2), scales=hq_s[:, 64 * u : 64 * (u + 1)],
+                                  in_=hid[:, 256 * u : 256 * (u + 1)])
+        for h in range(N // P):
+            cols = slice(P * h, P * (h + 1))
+            nc.tensor.matmul_mx(out=y_ps[h][:], lhsT=wb_w[:, cols].bitcast(E4M3), lhsT_scale=wb_s[:, cols],
+                                rhs=hq_w[:].bitcast(E5M2), rhs_scale=hq_s[:], start=False, stop=True)
+        for h in range(N // P):
+            y_sb = sb("y_sb%d" % h, O, F32)
+            leave_psum(h == 1, y_sb[:], y_ps[h][:])
+            (nc.sync, nc.scalar)[h].dma_start(out=out[P * h : P * (h + 1), :], in_=y_sb[:])

@@ -81,7 +81,9 @@ def tile_list_twow_agree_skip_plain_kernel(tc, xt_words, xt_scales, w_words, w_s
         load_scales((S, S, S, S), ws_s, ws_scales)
         load_scales((S, S, S, S), sx_s, sx_scales)
         load_scales((S, S, S, S), wb_s, wb_scales)
-
+        warm = keep.tile([P, 2], F32, name="warm")
+        nc.vector.memset(warm[:, 0:1], 0.0)
+        nc.scalar.activation(out=warm[:, 1:2], in_=warm[:, 0:1], func=ACT.Sigmoid)
         xg_w = sb("xg_w", J, U16)
         xg_s = sb("xg_s", J, U8)
         wd_w = sb("wd_w", R, U32)

@@ -57,24 +57,29 @@ def tile_list_twow_agree_skip_plain_kernel(tc, xt_words, xt_scales, w_words, w_s
                 queues[q].dma_start(out=tile[32 * q : 32 * q + 32, :].bitcast(I32),
                                     in_=rows.unsqueeze(0).to_broadcast([8, 4, rows.shape[1]]))
 
+        def spread_quadrant(queue, tile, scales, q):
+            rows = scales[0, 4 * q : 4 * q + 4, :].bitcast(I32)
+            queue.dma_start(out=tile[32 * q : 32 * q + 32, :].bitcast(I32),
+                            in_=rows.unsqueeze(0).to_broadcast([8, 4, rows.shape[1]]))
+
         def load_scales(queues, tile, scales):
             for q in range(4):
                 queues[q].dma_start(out=tile[32 * q : 32 * q + 4, :].bitcast(I32),
                                     in_=scales[0, 4 * q : 4 * q + 4, :].bitcast(I32))
 
-        for plane in (ws_s, sx_s, wb_s):
+        for plane in (w_s, w2_s, ws_s, sx_s, wb_s):
             nc.vector.memset(plane[:].bitcast(I32), 0)
         S, A, G = nc.sync, nc.scalar, nc.gpsimd
         spread_scales((S, A, S, A), xt_s, xt_scales)
         S.dma_start(list1[:], offs)
         A.dma_start(out=xt_w[:].bitcast(I32), in_=xt_words[0].bitcast(I32))
-        load_words(A, w2_w, w2_words)
+        load_words(S, w2_w, w2_words)
         load_words(A, w_w, w_words)
-        spread_scales((S, S, S, S), w2_s, w2_scales)
+        load_scales((S, S, S, S), w2_s, w2_scales)
+        load_scales((G, G, S, S), w_s, w_scales)
         S.dma_start(list2[:], offs2)
         S.dma_start(list3[:], offs3)
-        spread_scales((G, G, S, S), w_s, w_scales)
-        G.dma_start(out=slope[:], in_=sg.rearrange("(p t) one -> p (t one)", t=PACK))
+        S.dma_start(out=slope[:], in_=sg.rearrange("(p t) one -> p (t one)", t=PACK))
         load_words(S, ws_w, ws_words)
         load_words(S, sx_w, sx_words)
         load_words(S, wb_w, wb_words)
@@ -96,11 +101,13 @@ def tile_list_twow_agree_skip_plain_kernel(tc, xt_words, xt_scales, w_words, w_s
                     src.rearrange("p (c i t) -> p c t i", t=PACK, i=run))
 
         def deal_words_scalar(dst, src):
-            d, s = deal_views(dst[:], src[:], 4)
+            d = dst[:].rearrange("p (u e c i) -> p c u i e", u=2, e=2, i=4)
+            s = src[:].rearrange("p (c i u e) -> p c u i e", u=2, e=2, i=4)
             nc.scalar.copy(out=d, in_=s)
 
         def deal_words_vector(dst, src):
-            d, s = deal_views(dst[:].bitcast(I32), src[:].bitcast(I32), 4)
+            d = dst[:].bitcast(I32).rearrange("p (u e c i) -> p c u i e", u=2, e=2, i=4)
+            s = src[:].bitcast(I32).rearrange("p (c i u e) -> p c u i e", u=2, e=2, i=4)
             nc.vector.tensor_copy(out=d, in_=s)
 
         def deal_scales(engine, dst, src):
@@ -110,8 +117,10 @@ def tile_list_twow_agree_skip_plain_kernel(tc, xt_words, xt_scales, w_words, w_s
         nc.vector.tensor_copy(out=xg_s[:], in_=xt_s[:].indirect(list1[:]))
         nc.vector.tensor_copy(out=xg_w[:], in_=xt_w[:].indirect(list1[:]))
         deal_words_scalar(w2d_w, w2_w)
-        deal_scales(nc.vector, w2d_s, w2_s)
-        deal_words_vector(wd_w, w_w)
+        d, s = deal_views(w2d_s[:], w2_s[:], 16)
+        nc.vector.tensor_copy(out=d[:, :, 0, :], in_=s[:, :, 0, :])
+        nc.vector.tensor_copy(out=d[:, :, 1:4, :], in_=s[:, :, 1:4, :])
+        deal_words_scalar(wd_w, w_w)
         deal_scales(nc.vector, wd_s, w_s)
 
         def first_stage(name, words, scales, fmt, t):
@@ -176,10 +185,14 @@ def tile_list_twow_agree_skip_plain_kernel(tc, xt_words, xt_scales, w_words, w_s
             out_b(t, True)
             pick2(t, False)
             pick3(t, False)
-            larger(t)
         for t in range(PACK):
             out_a(t, True)
             look(t)
+        both = picked[:].rearrange("p (w t o) -> p w t o", w=2, t=PACK)
+        for u in range(2):
+            half = slice(64 * u, 64 * (u + 1))
+            nc.vector.tensor_tensor(out=top[:].rearrange("p (t o) -> p t o", t=PACK)[:, :, half], in0=both[:, 0, :, half],
+                                    in1=both[:, 1, :, half], op=ALU.max)
 
         hid = sb("hid", PACK * O, BF16)
         hq_w = sb("hq_w", O, U32)
@@ -191,11 +204,11 @@ def tile_list_twow_agree_skip_plain_kernel(tc, xt_words, xt_scales, w_words, w_s
             nc.tensor.matmul_mx(out=acc[:], lhsT=ws_w[:, cols].bitcast(E4M3), lhsT_scale=ws_s[:, cols],
                                 rhs=sx_w[:].bitcast(E5M2), rhs_scale=sx_s[:], start=True, stop=False)
             y_ps.append(acc)
-        hid_v = hid[:].rearrange("p (c i t) -> p c t i", t=PACK, i=4)
-        top_v = top[:].rearrange("p (t c i) -> p c t i", t=PACK, i=4)
-        gate_v = gate[:].rearrange("p (t c i) -> p c t i", t=PACK, i=4)
+        hid_v = hid[:].rearrange("p (c i t) -> p c t i", t=PACK, i=2)
+        top_v = top[:].rearrange("p (t c i) -> p c t i", t=PACK, i=2)
+        gate_v = gate[:].rearrange("p (t c i) -> p c t i", t=PACK, i=2)
         for u in range(2):
-            part = slice(16 * u, 16 * (u + 1))
+            part = slice(32 * u, 32 * (u + 1))
             nc.vector.tensor_tensor(out=hid_v[:, part], in0=top_v[:, part], in1=gate_v[:, part], op=ALU.mult)
         for u in range(2):
             nc.vector.quantize_mx(out=hq_w[:, 64 * u : 64 * (u + 1)].bitcast(E5M2), scales=hq_s[:, 64 * u : 64 * (u + 1)],

@@ -67,19 +67,21 @@ def tile_list_twow_agree_skip_plain_kernel(tc, xt_words, xt_scales, w_words, w_s
                 queues[q].dma_start(out=tile[32 * q : 32 * q + 4, :].bitcast(I32),
                                     in_=scales[0, 4 * q : 4 * q + 4, :].bitcast(I32))
 
-        for plane in (w_s, w2_s, ws_s, sx_s, wb_s):
+        for plane in (ws_s, sx_s, wb_s):
             nc.vector.memset(plane[:].bitcast(I32), 0)
         S, A, G = nc.sync, nc.scalar, nc.gpsimd
         spread_scales((S, A, S, A), xt_s, xt_scales)
         S.dma_start(list1[:], offs)
-        A.dma_start(out=xt_w[:].bitcast(I32), in_=xt_words[0].bitcast(I32))
-        load_words(S, w2_w, w2_words)
-        load_words(A, w_w, w_words)
-        load_scales((S, S, S, S), w2_s, w2_scales)
-        load_scales((G, G, S, S), w_s, w_scales)
+        spread_quadrant(A, w2_s, w2_scales, 0)
+        S.dma_start(out=xt_w[:].bitcast(I32), in_=xt_words[0].bitcast(I32))
+        load_words(A, w2_w, w2_words)
+        for q in (1, 2, 3):
+            spread_quadrant(S, w2_s, w2_scales, q)
+        load_words(S, w_w, w_words)
+        spread_scales((G, G, S, S), w_s, w_scales)
         S.dma_start(list2[:], offs2)
         S.dma_start(list3[:], offs3)
-        S.dma_start(out=slope[:], in_=sg.rearrange("(p t) one -> p (t one)", t=PACK))
+        G.dma_start(out=slope[:], in_=sg.rearrange("(p t) one -> p (t one)", t=PACK))
         load_words(S, ws_w, ws_words)
         load_words(S, sx_w, sx_words)
         load_words(S, wb_w, wb_words)
@@ -120,7 +122,7 @@ def tile_list_twow_agree_skip_plain_kernel(tc, xt_words, xt_scales, w_words, w_s
         d, s = deal_views(w2d_s[:], w2_s[:], 16)
         nc.vector.tensor_copy(out=d[:, :, 0, :], in_=s[:, :, 0, :])
         nc.vector.tensor_copy(out=d[:, :, 1:4, :], in_=s[:, :, 1:4, :])
-        deal_words_scalar(wd_w, w_w)
+        deal_words_vector(wd_w, w_w)
         deal_scales(nc.vector, wd_s, w_s)
 
         def first_stage(name, words, scales, fmt, t):
@@ -185,14 +187,10 @@ def tile_list_twow_agree_skip_plain_kernel(tc, xt_words, xt_scales, w_words, w_s
             out_b(t, True)
             pick2(t, False)
             pick3(t, False)
+            larger(t)
         for t in range(PACK):
             out_a(t, True)
             look(t)
-        both = picked[:].rearrange("p (w t o) -> p w t o", w=2, t=PACK)
-        for u in range(2):
-            half = slice(64 * u, 64 * (u + 1))
-            nc.vector.tensor_tensor(out=top[:].rearrange("p (t o) -> p t o", t=PACK)[:, :, half], in0=both[:, 0, :, half],
-                                    in1=both[:, 1, :, half], op=ALU.max)
 
         hid = sb("hid", PACK * O, BF16)
         hq_w = sb("hq_w", O, U32)

@@ -17,6 +17,9 @@ ALU = mybir.AluOpType
 K, T, J, R, O, N, L = 512, 1024, 256, 512, 128, 256, 512
 P = 128
 PACK = 4
+QUADRANTS = 4
+LIST_ROWS = 16
+PSUM_BANKS = 8
 FLOPS = 2 * (2 * K * R * J + R * N * O + L * N * O)
 
 
@@ -26,14 +29,14 @@ def tile_list_twow_agree_skip_plain_kernel(tc, xt_words, xt_scales, w_words, w_s
     nc = tc.nc
     with ExitStack() as ctx:
         keep = ctx.enter_context(tc.tile_pool(name="keep", bufs=1))
-        psum = ctx.enter_context(tc.psum_pool(name="psum", bufs=8))
+        psum = ctx.enter_context(tc.psum_pool(name="psum", bufs=PSUM_BANKS))
 
         def sb(name, cols, dtype, tag=None):
             return keep.tile([P, cols], dtype, name=name, tag=tag or name, align_bytes=64)
 
-        list1 = keep.tile([P, J // 16], U16, name="list1")
-        list2 = keep.tile([P, O // 16], U16, name="list2")
-        list3 = keep.tile([P, O // 16], U16, name="list3")
+        list1 = keep.tile([P, J // LIST_ROWS], U16, name="list1")
+        list2 = keep.tile([P, O // LIST_ROWS], U16, name="list2")
+        list3 = keep.tile([P, O // LIST_ROWS], U16, name="list3")
         xt_w = sb("xt_w", T, U16)
         xt_s = sb("xt_s", T, U8)
         w_w = sb("w_w", R, U32)
@@ -51,98 +54,81 @@ def tile_list_twow_agree_skip_plain_kernel(tc, xt_words, xt_scales, w_words, w_s
         def load_words(queue, tile, words):
             queue.dma_start(out=tile[:].bitcast(I32), in_=words[0].rearrange("p n t -> p (n t)").bitcast(I32))
 
-        def spread_scales(queues, tile, scales):
-            for q in range(4):
-                rows = scales[0, 4 * q : 4 * q + 4, :].bitcast(I32)
-                queues[q].dma_start(out=tile[32 * q : 32 * q + 32, :].bitcast(I32),
-                                    in_=rows.unsqueeze(0).to_broadcast([8, 4, rows.shape[1]]))
-
-        def spread_quadrant(queue, tile, scales, q):
+        def fill_quadrant(queue, plane, scales, q):
             rows = scales[0, 4 * q : 4 * q + 4, :].bitcast(I32)
-            queue.dma_start(out=tile[32 * q : 32 * q + 32, :].bitcast(I32),
+            queue.dma_start(out=plane[32 * q : 32 * q + 32, :].bitcast(I32),
                             in_=rows.unsqueeze(0).to_broadcast([8, 4, rows.shape[1]]))
 
-        def load_scales(queues, tile, scales):
-            for q in range(4):
-                queues[q].dma_start(out=tile[32 * q : 32 * q + 4, :].bitcast(I32),
-                                    in_=scales[0, 4 * q : 4 * q + 4, :].bitcast(I32))
+        def fill_plane(queues, plane, scales):
+            for q in range(QUADRANTS):
+                fill_quadrant(queues[q], plane, scales, q)
+
+        def load_plane(plane, scales):
+            for q in range(QUADRANTS):
+                nc.sync.dma_start(out=plane[32 * q : 32 * q + 4, :].bitcast(I32),
+                                  in_=scales[0, 4 * q : 4 * q + 4, :].bitcast(I32))
 
         for plane in (ws_s, sx_s, wb_s):
             nc.vector.memset(plane[:].bitcast(I32), 0)
-        S, A, G = nc.sync, nc.scalar, nc.gpsimd
-        spread_scales((S, A, S, A), xt_s, xt_scales)
-        S.dma_start(list1[:], offs)
-        spread_quadrant(A, w2_s, w2_scales, 0)
-        S.dma_start(out=xt_w[:].bitcast(I32), in_=xt_words[0].bitcast(I32))
-        load_words(A, w2_w, w2_words)
-        for q in (1, 2, 3):
-            spread_quadrant(S, w2_s, w2_scales, q)
-        load_words(S, w_w, w_words)
-        spread_scales((G, G, S, S), w_s, w_scales)
-        S.dma_start(list2[:], offs2)
-        S.dma_start(list3[:], offs3)
-        G.dma_start(out=slope[:], in_=sg.rearrange("(p t) one -> p (t one)", t=PACK))
-        load_words(S, ws_w, ws_words)
-        load_words(S, sx_w, sx_words)
-        load_words(S, wb_w, wb_words)
-        load_scales((S, S, S, S), ws_s, ws_scales)
-        load_scales((S, S, S, S), sx_s, sx_scales)
-        load_scales((S, S, S, S), wb_s, wb_scales)
+
+        sync, scalar, gpsimd = nc.sync, nc.scalar, nc.gpsimd
+        fill_plane((sync, scalar, sync, scalar), xt_s, xt_scales)
+        sync.dma_start(list1[:], offs)
+        fill_quadrant(scalar, w2_s, w2_scales, 0)
+        sync.dma_start(out=xt_w[:].bitcast(I32), in_=xt_words[0].bitcast(I32))
+        load_words(scalar, w2_w, w2_words)
+        fill_quadrant(sync, w2_s, w2_scales, 1)
+        fill_quadrant(sync, w2_s, w2_scales, 2)
+        fill_quadrant(gpsimd, w2_s, w2_scales, 3)
+        load_words(sync, w_w, w_words)
+        fill_plane((gpsimd, sync, sync, sync), w_s, w_scales)
+        sync.dma_start(list2[:], offs2)
+        sync.dma_start(list3[:], offs3)
+        gpsimd.dma_start(out=slope[:], in_=sg.rearrange("(p t) one -> p (t one)", t=PACK))
+        load_words(sync, ws_w, ws_words)
+        load_words(sync, sx_w, sx_words)
+        load_words(sync, wb_w, wb_words)
+        load_plane(ws_s, ws_scales)
+        load_plane(sx_s, sx_scales)
+        load_plane(wb_s, wb_scales)
+
         warm = keep.tile([P, 2], F32, name="warm")
         nc.vector.memset(warm[:, 0:1], 0.0)
         nc.scalar.activation(out=warm[:, 1:2], in_=warm[:, 0:1], func=ACT.Sigmoid)
+
         xg_w = sb("xg_w", J, U16)
         xg_s = sb("xg_s", J, U8)
         wd_w = sb("wd_w", R, U32)
         wd_s = sb("wd_s", R, U8)
         w2d_w = sb("w2d_w", R, U32)
         w2d_s = sb("w2d_s", R, U8)
-
-        def deal_views(dst, src, run):
-            return (dst.rearrange("p (t c i) -> p c t i", t=PACK, i=run),
-                    src.rearrange("p (c i t) -> p c t i", t=PACK, i=run))
-
-        def deal_words_scalar(dst, src):
-            d = dst[:].rearrange("p (u e c i) -> p c u i e", u=2, e=2, i=4)
-            s = src[:].rearrange("p (c i u e) -> p c u i e", u=2, e=2, i=4)
-            nc.scalar.copy(out=d, in_=s)
-
-        def deal_words_vector(dst, src):
-            d = dst[:].bitcast(I32).rearrange("p (u e c i) -> p c u i e", u=2, e=2, i=4)
-            s = src[:].bitcast(I32).rearrange("p (c i u e) -> p c u i e", u=2, e=2, i=4)
-            nc.vector.tensor_copy(out=d, in_=s)
-
-        def deal_scales(engine, dst, src):
-            d, s = deal_views(dst[:], src[:], 16)
-            engine.tensor_copy(out=d, in_=s)
-
         nc.vector.tensor_copy(out=xg_s[:], in_=xt_s[:].indirect(list1[:]))
         nc.vector.tensor_copy(out=xg_w[:], in_=xt_w[:].indirect(list1[:]))
-        deal_words_scalar(w2d_w, w2_w)
-        d, s = deal_views(w2d_s[:], w2_s[:], 16)
-        nc.vector.tensor_copy(out=d[:, :, 0, :], in_=s[:, :, 0, :])
-        nc.vector.tensor_copy(out=d[:, :, 1:4, :], in_=s[:, :, 1:4, :])
-        deal_words_vector(wd_w, w_w)
-        deal_scales(nc.vector, wd_s, w_s)
 
-        def first_stage(name, words, scales, fmt, t):
-            acc = psum.tile([P, J], F32, name=name, tag="acc")
+        def word_deal(dst, src):
+            return (dst.rearrange("p (u e c i) -> p c u i e", u=2, e=2, i=4),
+                    src.rearrange("p (c i u e) -> p c u i e", u=2, e=2, i=4))
+
+        def byte_deal(dst, src):
+            return (dst.rearrange("p (t c i) -> p c t i", t=PACK, i=16),
+                    src.rearrange("p (c i t) -> p c t i", t=PACK, i=16))
+
+        dst, src = word_deal(w2d_w[:], w2_w[:])
+        nc.scalar.copy(out=dst, in_=src)
+        dst, src = byte_deal(w2d_s[:], w2_s[:])
+        nc.vector.tensor_copy(out=dst[:, :, 0, :], in_=src[:, :, 0, :])
+        nc.vector.tensor_copy(out=dst[:, :, 1:PACK, :], in_=src[:, :, 1:PACK, :])
+        dst, src = word_deal(wd_w[:].bitcast(I32), w_w[:].bitcast(I32))
+        nc.vector.tensor_copy(out=dst, in_=src)
+        dst, src = byte_deal(wd_s[:], w_s[:])
+        nc.vector.tensor_copy(out=dst, in_=src)
+
+        def first_stage(name, words, scales, fmt, t, tokens):
+            acc = psum.tile([P, tokens.stop - tokens.start], F32, name=name, tag="acc")
             cols = slice(P * t, P * (t + 1))
             nc.tensor.matmul_mx(out=acc[:], lhsT=words[:, cols].bitcast(fmt), lhsT_scale=scales[:, cols],
-                                rhs=xg_w[:].bitcast(E2M1), rhs_scale=xg_s[:], start=True, stop=True)
+                                rhs=xg_w[:, tokens].bitcast(E2M1), rhs_scale=xg_s[:, tokens], start=True, stop=True)
             return acc
-
-        def leave_psum(on_scalar, dst, src):
-            if on_scalar:
-                nc.scalar.copy(out=dst, in_=src)
-            else:
-                nc.vector.tensor_copy(out=dst, in_=src)
-
-        def pick(on_scalar, dst, window, offsets):
-            if on_scalar:
-                nc.scalar.activation(out=dst, in_=window[:].indirect(offsets[:]), func=ACT.Copy)
-            else:
-                nc.vector.tensor_copy(out=dst, in_=window[:].indirect(offsets[:]))
 
         a_sb = [sb("a_sb%d" % t, J, F32) for t in range(PACK)]
         b_sb = [sb("b_sb%d" % t, J, F32) for t in range(PACK)]
@@ -151,46 +137,25 @@ def tile_list_twow_agree_skip_plain_kernel(tc, xt_words, xt_scales, w_words, w_s
         b3 = [picked[:, O * (PACK + t) : O * (PACK + t + 1)] for t in range(PACK)]
         gate = sb("gate", PACK * O, F32)
         top = sb("top", PACK * O, F32)
-        a_ps = {}
-        b_ps = {}
 
-        def mm_a(t):
-            a_ps[t] = first_stage("a_ps%d" % t, wd_w, wd_s, E5M2, t)
+        every = slice(0, J)
+        halves = (slice(0, J // 2), slice(J // 2, J))
+        b0_ps = [first_stage("b_ps0_%d" % u, w2d_w, w2d_s, E4M3, 0, half) for u, half in enumerate(halves)]
+        b_ps = {t: first_stage("b_ps%d" % t, w2d_w, w2d_s, E4M3, t, every) for t in range(1, PACK)}
+        for acc, half in zip(b0_ps, halves):
+            nc.scalar.copy(out=b_sb[0][:, half], in_=acc[:])
+        a_ps = [first_stage("a_ps%d" % t, wd_w, wd_s, E5M2, t, every) for t in range(PACK)]
 
-        def mm_b(t):
-            b_ps[t] = first_stage("b_ps%d" % t, w2d_w, w2d_s, E4M3, t)
-
-        def out_a(t, on_scalar):
-            leave_psum(on_scalar, a_sb[t][:], a_ps[t][:])
-
-        def out_b(t, on_scalar):
-            leave_psum(on_scalar, b_sb[t][:], b_ps[t][:])
-
-        def look(t):
+        for t in range(PACK):
+            if t in b_ps:
+                nc.scalar.copy(out=b_sb[t][:], in_=b_ps[t][:])
+            nc.vector.tensor_copy(out=b2[t], in_=b_sb[t][:].indirect(list2[:]))
+            nc.vector.tensor_copy(out=b3[t], in_=b_sb[t][:].indirect(list3[:]))
+            nc.vector.tensor_tensor(out=top[:, O * t : O * (t + 1)], in0=b2[t], in1=b3[t], op=ALU.max)
+        for t in range(PACK):
+            nc.scalar.copy(out=a_sb[t][:], in_=a_ps[t][:])
             nc.scalar.activation(out=gate[:, O * t : O * (t + 1)], in_=a_sb[t][:].indirect(list3[:]),
                                  func=ACT.Sigmoid, scale=slope[:, t : t + 1])
-
-        def pick2(t, on_scalar):
-            pick(on_scalar, b2[t], b_sb[t], list2)
-
-        def pick3(t, on_scalar):
-            pick(on_scalar, b3[t], b_sb[t], list3)
-
-        def larger(t):
-            nc.vector.tensor_tensor(out=top[:, O * t : O * (t + 1)], in0=b2[t], in1=b3[t], op=ALU.max)
-
-        for t in range(PACK):
-            mm_b(t)
-        for t in range(PACK):
-            mm_a(t)
-        for t in range(PACK):
-            out_b(t, True)
-            pick2(t, False)
-            pick3(t, False)
-            larger(t)
-        for t in range(PACK):
-            out_a(t, True)
-            look(t)
 
         hid = sb("hid", PACK * O, BF16)
         hq_w = sb("hq_w", O, U32)
@@ -202,20 +167,25 @@ def tile_list_twow_agree_skip_plain_kernel(tc, xt_words, xt_scales, w_words, w_s
             nc.tensor.matmul_mx(out=acc[:], lhsT=ws_w[:, cols].bitcast(E4M3), lhsT_scale=ws_s[:, cols],
                                 rhs=sx_w[:].bitcast(E5M2), rhs_scale=sx_s[:], start=True, stop=False)
             y_ps.append(acc)
+
         hid_v = hid[:].rearrange("p (c i t) -> p c t i", t=PACK, i=2)
         top_v = top[:].rearrange("p (t c i) -> p c t i", t=PACK, i=2)
         gate_v = gate[:].rearrange("p (t c i) -> p c t i", t=PACK, i=2)
         for u in range(2):
-            part = slice(32 * u, 32 * (u + 1))
-            nc.vector.tensor_tensor(out=hid_v[:, part], in0=top_v[:, part], in1=gate_v[:, part], op=ALU.mult)
+            pairs = slice(O // 4 * u, O // 4 * (u + 1))
+            nc.vector.tensor_tensor(out=hid_v[:, pairs], in0=top_v[:, pairs], in1=gate_v[:, pairs], op=ALU.mult)
         for u in range(2):
-            nc.vector.quantize_mx(out=hq_w[:, 64 * u : 64 * (u + 1)].bitcast(E5M2), scales=hq_s[:, 64 * u : 64 * (u + 1)],
-                                  in_=hid[:, 256 * u : 256 * (u + 1)])
+            places = slice(O // 2 * u, O // 2 * (u + 1))
+            nc.vector.quantize_mx(out=hq_w[:, places].bitcast(E5M2), scales=hq_s[:, places],
+                                  in_=hid[:, PACK * places.start : PACK * places.stop])
         for h in range(N // P):
             cols = slice(P * h, P * (h + 1))
             nc.tensor.matmul_mx(out=y_ps[h][:], lhsT=wb_w[:, cols].bitcast(E4M3), lhsT_scale=wb_s[:, cols],
                                 rhs=hq_w[:].bitcast(E5M2), rhs_scale=hq_s[:], start=False, stop=True)
-        for h in range(N // P):
-            y_sb = sb("y_sb%d" % h, O, F32)
-            leave_psum(h == 1, y_sb[:], y_ps[h][:])
-            (nc.sync, nc.scalar)[h].dma_start(out=out[P * h : P * (h + 1), :], in_=y_sb[:])
+
+        y0_sb = sb("y_sb0", O, F32)
+        nc.vector.tensor_copy(out=y0_sb[:], in_=y_ps[0][:])
+        sync.dma_start(out=out[0:P, :], in_=y0_sb[:])
+        y1_sb = sb("y_sb1", O, F32)
+        nc.scalar.copy(out=y1_sb[:], in_=y_ps[1][:])
+        scalar.dma_start(out=out[P : 2 * P, :], in_=y1_sb[:])

from contextlib import ExitStack

import concourse.mybir as mybir

F32 = mybir.dt.float32
BF16 = mybir.dt.bfloat16
I32 = mybir.dt.int32
U32 = mybir.dt.uint32
U16 = mybir.dt.uint16
U8 = mybir.dt.uint8
E4M3 = mybir.dt.float8_e4m3fn_x4
E5M2 = mybir.dt.float8_e5m2_x4
E2M1 = mybir.dt.float4_e2m1fn_x4
ACT = mybir.ActivationFunctionType
ALU = mybir.AluOpType

K, T, J, R, O, N, L = 512, 1024, 256, 512, 128, 256, 512
P = 128
PACK = 4
QUADRANTS = 4
LIST_ROWS = 16
PSUM_BANKS = 8
FLOPS = 2 * (2 * K * R * J + R * N * O + L * N * O)


def tile_list_twow_agree_skip_plain_kernel(tc, xt_words, xt_scales, w_words, w_scales, w2_words, w2_scales, sg,
                                                 wb_words, wb_scales, sx_words, sx_scales, ws_words, ws_scales,
                                                 offs, offs2, offs3, out):
    nc = tc.nc
    with ExitStack() as ctx:
        keep = ctx.enter_context(tc.tile_pool(name="keep", bufs=1))
        psum = ctx.enter_context(tc.psum_pool(name="psum", bufs=PSUM_BANKS))

        def sb(name, cols, dtype, tag=None):
            return keep.tile([P, cols], dtype, name=name, tag=tag or name, align_bytes=64)

        list1 = keep.tile([P, J // LIST_ROWS], U16, name="list1")
        list2 = keep.tile([P, O // LIST_ROWS], U16, name="list2")
        list3 = keep.tile([P, O // LIST_ROWS], U16, name="list3")
        xt_w = sb("xt_w", T, U16)
        xt_s = sb("xt_s", T, U8)
        w_w = sb("w_w", R, U32)
        w_s = sb("w_s", R, U8)
        w2_w = sb("w2_w", R, U32)
        w2_s = sb("w2_s", R, U8)
        wb_w = sb("wb_w", N, U32)
        wb_s = sb("wb_s", N, U8)
        ws_w = sb("ws_w", N, U32)
        ws_s = sb("ws_s", N, U8)
        sx_w = sb("sx_w", O, U32)
        sx_s = sb("sx_s", O, U8)
        slope = sb("slope", PACK, F32)

        def load_words(queue, tile, words):
            queue.dma_start(out=tile[:].bitcast(I32), in_=words[0].rearrange("p n t -> p (n t)").bitcast(I32))

        def fill_quadrant(queue, plane, scales, q):
            rows = scales[0, 4 * q : 4 * q + 4, :].bitcast(I32)
            queue.dma_start(out=plane[32 * q : 32 * q + 32, :].bitcast(I32),
                            in_=rows.unsqueeze(0).to_broadcast([8, 4, rows.shape[1]]))

        def fill_plane(queues, plane, scales):
            for q in range(QUADRANTS):
                fill_quadrant(queues[q], plane, scales, q)

        def load_plane(plane, scales):
            for q in range(QUADRANTS):
                nc.sync.dma_start(out=plane[32 * q : 32 * q + 4, :].bitcast(I32),
                                  in_=scales[0, 4 * q : 4 * q + 4, :].bitcast(I32))

        for plane in (ws_s, sx_s, wb_s):
            nc.vector.memset(plane[:].bitcast(I32), 0)

        sync, scalar, gpsimd = nc.sync, nc.scalar, nc.gpsimd
        fill_plane((sync, scalar, sync, scalar), xt_s, xt_scales)
        sync.dma_start(list1[:], offs)
        fill_quadrant(scalar, w2_s, w2_scales, 0)
        sync.dma_start(out=xt_w[:].bitcast(I32), in_=xt_words[0].bitcast(I32))
        load_words(scalar, w2_w, w2_words)
        fill_quadrant(sync, w2_s, w2_scales, 1)
        fill_quadrant(sync, w2_s, w2_scales, 2)
        fill_quadrant(gpsimd, w2_s, w2_scales, 3)
        load_words(sync, w_w, w_words)
        fill_plane((gpsimd, sync, sync, sync), w_s, w_scales)
        sync.dma_start(list2[:], offs2)
        sync.dma_start(list3[:], offs3)
        gpsimd.dma_start(out=slope[:], in_=sg.rearrange("(p t) one -> p (t one)", t=PACK))
        load_words(sync, ws_w, ws_words)
        load_words(sync, sx_w, sx_words)
        load_words(sync, wb_w, wb_words)
        load_plane(ws_s, ws_scales)
        load_plane(sx_s, sx_scales)
        load_plane(wb_s, wb_scales)

        warm = keep.tile([P, 2], F32, name="warm")
        nc.vector.memset(warm[:, 0:1], 0.0)
        nc.scalar.activation(out=warm[:, 1:2], in_=warm[:, 0:1], func=ACT.Sigmoid)

        xg_w = sb("xg_w", J, U16)
        xg_s = sb("xg_s", J, U8)
        wd_w = sb("wd_w", R, U32)
        wd_s = sb("wd_s", R, U8)
        w2d_w = sb("w2d_w", R, U32)
        w2d_s = sb("w2d_s", R, U8)
        nc.vector.tensor_copy(out=xg_s[:], in_=xt_s[:].indirect(list1[:]))
        nc.vector.tensor_copy(out=xg_w[:], in_=xt_w[:].indirect(list1[:]))

        def word_deal(dst, src):
            return (dst.rearrange("p (u e c i) -> p c u i e", u=2, e=2, i=4),
                    src.rearrange("p (c i u e) -> p c u i e", u=2, e=2, i=4))

        def byte_deal(dst, src):
            return (dst.rearrange("p (t c i) -> p c t i", t=PACK, i=16),
                    src.rearrange("p (c i t) -> p c t i", t=PACK, i=16))

        dst, src = word_deal(w2d_w[:], w2_w[:])
        nc.scalar.copy(out=dst, in_=src)
        dst, src = byte_deal(w2d_s[:], w2_s[:])
        nc.vector.tensor_copy(out=dst[:, :, 0, :], in_=src[:, :, 0, :])
        nc.vector.tensor_copy(out=dst[:, :, 1:PACK, :], in_=src[:, :, 1:PACK, :])
        dst, src = word_deal(wd_w[:].bitcast(I32), w_w[:].bitcast(I32))
        nc.vector.tensor_copy(out=dst, in_=src)
        dst, src = byte_deal(wd_s[:], w_s[:])
        nc.vector.tensor_copy(out=dst, in_=src)

        def first_stage(name, words, scales, fmt, t, tokens):
            acc = psum.tile([P, tokens.stop - tokens.start], F32, name=name, tag="acc")
            cols = slice(P * t, P * (t + 1))
            nc.tensor.matmul_mx(out=acc[:], lhsT=words[:, cols].bitcast(fmt), lhsT_scale=scales[:, cols],
                                rhs=xg_w[:, tokens].bitcast(E2M1), rhs_scale=xg_s[:, tokens], start=True, stop=True)
            return acc

        a_sb = [sb("a_sb%d" % t, J, F32) for t in range(PACK)]
        b_sb = [sb("b_sb%d" % t, J, F32) for t in range(PACK)]
        picked = sb("picked", 2 * PACK * O, F32, "w_s")
        b2 = [picked[:, O * t : O * (t + 1)] for t in range(PACK)]
        b3 = [picked[:, O * (PACK + t) : O * (PACK + t + 1)] for t in range(PACK)]
        gate = sb("gate", PACK * O, F32)
        top = sb("top", PACK * O, F32)

        every = slice(0, J)
        halves = (slice(0, J // 2), slice(J // 2, J))
        b0_ps = [first_stage("b_ps0_%d" % u, w2d_w, w2d_s, E4M3, 0, half) for u, half in enumerate(halves)]
        b_ps = {t: first_stage("b_ps%d" % t, w2d_w, w2d_s, E4M3, t, every) for t in range(1, PACK)}
        for acc, half in zip(b0_ps, halves):
            nc.scalar.copy(out=b_sb[0][:, half], in_=acc[:])
        a_ps = [first_stage("a_ps%d" % t, wd_w, wd_s, E5M2, t, every) for t in range(PACK)]

        for t in range(PACK):
            if t in b_ps:
                nc.scalar.copy(out=b_sb[t][:], in_=b_ps[t][:])
            nc.vector.tensor_copy(out=b2[t], in_=b_sb[t][:].indirect(list2[:]))
            nc.vector.tensor_copy(out=b3[t], in_=b_sb[t][:].indirect(list3[:]))
            nc.vector.tensor_tensor(out=top[:, O * t : O * (t + 1)], in0=b2[t], in1=b3[t], op=ALU.max)
        for t in range(PACK):
            nc.scalar.copy(out=a_sb[t][:], in_=a_ps[t][:])
            nc.scalar.activation(out=gate[:, O * t : O * (t + 1)], in_=a_sb[t][:].indirect(list3[:]),
                                 func=ACT.Sigmoid, scale=slope[:, t : t + 1])

        hid = sb("hid", PACK * O, BF16)
        hq_w = sb("hq_w", O, U32)
        hq_s = sb("hq_s", O, U8)
        y_ps = []
        for h in range(N // P):
            acc = psum.tile([P, O], F32, name="y_ps%d" % h, tag="acc")
            cols = slice(P * h, P * (h + 1))
            nc.tensor.matmul_mx(out=acc[:], lhsT=ws_w[:, cols].bitcast(E4M3), lhsT_scale=ws_s[:, cols],
                                rhs=sx_w[:].bitcast(E5M2), rhs_scale=sx_s[:], start=True, stop=False)
            y_ps.append(acc)

        hid_v = hid[:].rearrange("p (c i t) -> p c t i", t=PACK, i=2)
        top_v = top[:].rearrange("p (t c i) -> p c t i", t=PACK, i=2)
        gate_v = gate[:].rearrange("p (t c i) -> p c t i", t=PACK, i=2)
        for u in range(2):
            pairs = slice(O // 4 * u, O // 4 * (u + 1))
            nc.vector.tensor_tensor(out=hid_v[:, pairs], in0=top_v[:, pairs], in1=gate_v[:, pairs], op=ALU.mult)
        for u in range(2):
            places = slice(O // 2 * u, O // 2 * (u + 1))
            nc.vector.quantize_mx(out=hq_w[:, places].bitcast(E5M2), scales=hq_s[:, places],
                                  in_=hid[:, PACK * places.start : PACK * places.stop])
        for h in range(N // P):
            cols = slice(P * h, P * (h + 1))
            nc.tensor.matmul_mx(out=y_ps[h][:], lhsT=wb_w[:, cols].bitcast(E4M3), lhsT_scale=wb_s[:, cols],
                                rhs=hq_w[:].bitcast(E5M2), rhs_scale=hq_s[:], start=False, stop=True)

        y0_sb = sb("y_sb0", O, F32)
        nc.vector.tensor_copy(out=y0_sb[:], in_=y_ps[0][:])
        sync.dma_start(out=out[0:P, :], in_=y0_sb[:])
        y1_sb = sb("y_sb1", O, F32)
        nc.scalar.copy(out=y1_sb[:], in_=y_ps[1][:])
        scalar.dma_start(out=out[P : 2 * P, :], in_=y1_sb[:])
